import numpy as np
import ml_dtypes

BF16 = ml_dtypes.bfloat16


def bf(x):
    return np.asarray(x, np.float32).astype(BF16)


def f32(x):
    return np.asarray(x, np.float32)


def f64(x):
    return np.asarray(x).astype(np.float64)


def striped(idx):
    return np.tile(idx.reshape(-1, 16).T, (8, 1))


S, K, M, N, V, D = 512, 256, 512, 128, 32, 16


def setup_inputs():
    return {"base": bf(np.random.standard_normal((M, S))), "x": bf(np.random.standard_normal((K, N))), "w": bf(1.5 * np.random.standard_normal((K, M)) / np.sqrt(K)), "offs": striped(np.random.permutation(S)[:N])}


def reference(base, x, w, offs):
    idx = offs[:16].T.reshape(-1)
    z = f64(base).copy()
    z[:, idx] += f64(w).T @ f64(x)
    u = z.reshape(M, V, D)
    u = u - u.max(axis=2, keepdims=True)
    u = np.exp(u)
    u = u / u.sum(axis=2, keepdims=True)
    return u.reshape(M, S)

@@ -1,0 +1,72 @@
+import concourse.mybir as mybir
+from concourse.masks import make_identity
+
+P = 128
+STATES, WORDS = 512, 512
+FEATURES, CANDIDATES = 256, 128
+SLATE = 16
+SLATES = WORDS // SLATE
+BLOCKS = STATES // P
+K_BLOCKS = FEATURES // P
+
+FLOPS = 2 * FEATURES * STATES * CANDIDATES + 5 * STATES * WORDS
+
+BF16, F32, U16 = mybir.dt.bfloat16, mybir.dt.float32, mybir.dt.uint16
+X_AXIS = mybir.AxisListType.X
+OP = mybir.AluOpType
+EXP = mybir.ActivationFunctionType.Exp
+
+
+def spread(per_slate):
+    return per_slate.unsqueeze(2).to_broadcast([P, SLATES, SLATE])
+
+
+def tile_rows_rescore_kernel(tc, base, x, w, offs, out):
+    nc = tc.nc
+    with (
+        tc.tile_pool(name="held", bufs=1) as held,
+        tc.tile_pool(name="work", bufs=BLOCKS) as work,
+        tc.psum_pool(name="windows", bufs=1) as windows,
+    ):
+        base_rows = [held.tile([P, WORDS], BF16, name=f"base_rows{b}") for b in range(BLOCKS)]
+        for b in range(BLOCKS):
+            nc.sync.dma_start(base_rows[b][:], base[b * P : (b + 1) * P, :])
+        offsets = held.tile([P, CANDIDATES // 16], U16, name="offsets")
+        nc.sync.dma_start(offsets[:], offs)
+        x_blocks = held.tile([P, K_BLOCKS, CANDIDATES], BF16, name="x_blocks")
+        nc.scalar.dma_start(x_blocks[:], x.rearrange("(a p) n -> p a n", p=P))
+        w_blocks = held.tile([P, K_BLOCKS, STATES], BF16, name="w_blocks")
+        nc.scalar.dma_start(w_blocks[:], w.rearrange("(a p) m -> p a m", p=P))
+
+        identity = held.tile([P, P], BF16, name="identity")
+        make_identity(nc, identity[:])
+
+        window = [windows.tile([P, WORDS], F32, name=f"window{b}") for b in range(BLOCKS)]
+        for b in range(BLOCKS):
+            nc.tensor.matmul(window[b][:], identity[:], base_rows[b][:], start=True, stop=False)
+
+        for b in range(BLOCKS):
+            for a in range(K_BLOCKS):
+                nc.tensor.matmul(
+                    window[b][:].indirect(offsets[:]),
+                    w_blocks[:, a, b * P : (b + 1) * P],
+                    x_blocks[:, a, :],
+                    start=False,
+                    stop=a == K_BLOCKS - 1,
+                )
+
+        for b in range(BLOCKS):
+            z = window[b][:].rearrange("p (v d) -> p v d", d=SLATE)
+            slate_max = work.tile([P, SLATES], F32, name="slate_max")
+            nc.vector.tensor_reduce(slate_max[:], z, X_AXIS, OP.max)
+            shifted = work.tile([P, SLATES, SLATE], F32, name="shifted")
+            nc.vector.tensor_tensor(shifted[:], z, spread(slate_max[:]), OP.subtract)
+            exps = work.tile([P, SLATES, SLATE], F32, name="exps")
+            nc.scalar.activation(exps[:], shifted[:], EXP)
+            slate_sum = work.tile([P, SLATES], F32, name="slate_sum")
+            nc.vector.tensor_reduce(slate_sum[:], exps[:], X_AXIS, OP.add)
+            inverse = work.tile([P, SLATES], F32, name="inverse")
+            nc.vector.reciprocal(inverse[:], slate_sum[:])
+            probs = work.tile([P, SLATES, SLATE], F32, name="probs")
+            nc.vector.tensor_tensor(probs[:], exps[:], spread(inverse[:]), OP.mult)
+            nc.sync.dma_start(out[b * P : (b + 1) * P, :], probs[:].rearrange("p v d -> p (v d)"))

@@ -68,5 +68,6 @@ def tile_rows_rescore_kernel(tc, base, x, w, offs, out):
             inverse = work.tile([P, SLATES], F32, name="inverse")
             nc.vector.reciprocal(inverse[:], slate_sum[:])
             probs = work.tile([P, SLATES, SLATE], F32, name="probs")
-            nc.vector.tensor_tensor(probs[:], exps[:], spread(inverse[:]), OP.mult)
+            normaliser = nc.gpsimd if b < BLOCKS - 1 else nc.vector
+            normaliser.tensor_tensor(probs[:], exps[:], spread(inverse[:]), OP.mult)
             nc.sync.dma_start(out[b * P : (b + 1) * P, :], probs[:].rearrange("p v d -> p (v d)"))

@@ -9,6 +9,10 @@ SLATES = WORDS // SLATE
 BLOCKS = STATES // P
 K_BLOCKS = FEATURES // P
 
+WARM_UPS = 3
+SEPARATORS = 24
+PIECES = SEPARATORS // (BLOCKS - 1)
+
 FLOPS = 2 * FEATURES * STATES * CANDIDATES + 5 * STATES * WORDS
 
 BF16, F32, U16 = mybir.dt.bfloat16, mybir.dt.float32, mybir.dt.uint16
@@ -21,6 +25,10 @@ def spread(per_slate):
     return per_slate.unsqueeze(2).to_broadcast([P, SLATES, SLATE])
 
 
+def by_slate(row):
+    return row.rearrange("p (v d) -> p v d", d=SLATE)
+
+
 def tile_rows_rescore_kernel(tc, base, x, w, offs, out):
     nc = tc.nc
     with (
@@ -29,45 +37,102 @@ def tile_rows_rescore_kernel(tc, base, x, w, offs, out):
         tc.psum_pool(name="windows", bufs=1) as windows,
     ):
         base_rows = [held.tile([P, WORDS], BF16, name=f"base_rows{b}") for b in range(BLOCKS)]
-        for b in range(BLOCKS):
-            nc.sync.dma_start(base_rows[b][:], base[b * P : (b + 1) * P, :])
         offsets = held.tile([P, CANDIDATES // 16], U16, name="offsets")
-        nc.sync.dma_start(offsets[:], offs)
         x_blocks = held.tile([P, K_BLOCKS, CANDIDATES], BF16, name="x_blocks")
-        nc.scalar.dma_start(x_blocks[:], x.rearrange("(a p) n -> p a n", p=P))
-        w_blocks = held.tile([P, K_BLOCKS, STATES], BF16, name="w_blocks")
-        nc.scalar.dma_start(w_blocks[:], w.rearrange("(a p) m -> p a m", p=P))
+        w_blocks = [held.tile([P, K_BLOCKS, P], BF16, name="w_first")]
+        w_rest = held.tile([P, K_BLOCKS, STATES - P], BF16, name="w_rest")
+        w_blocks += [w_rest[:, :, (b - 1) * P : b * P] for b in range(1, BLOCKS)]
+        nc.sync.dma_start(base_rows[0][:], base[:P, :])
+        nc.sync.dma_start(x_blocks[:], x.rearrange("(a p) n -> p a n", p=P))
+        w_by_feature = w.rearrange("(a p) m -> p a m", p=P)
+        nc.sync.dma_start(w_blocks[0][:], w_by_feature[:, :, :P])
+        nc.sync.dma_start(offsets[:], offs)
+        for b in range(1, BLOCKS):
+            nc.sync.dma_start(base_rows[b][:], base[b * P : (b + 1) * P, :])
+        nc.sync.dma_start(w_rest[:], w_by_feature[:, :, P:])
 
+        zero = held.tile([P, 1], F32, name="zero")
+        nc.vector.memset(zero[:], 0.0)
+        one = held.tile([P, 1], F32, name="one")
+        nc.scalar.activation(one[:], zero[:], EXP)
+
+        zeros = held.tile([P, WORDS], BF16, name="zeros")
+        nc.gpsimd.memset(zeros[:], 0.0)
         identity = held.tile([P, P], BF16, name="identity")
         make_identity(nc, identity[:])
 
-        window = [windows.tile([P, WORDS], F32, name=f"window{b}") for b in range(BLOCKS)]
-        for b in range(BLOCKS):
-            nc.tensor.matmul(window[b][:], identity[:], base_rows[b][:], start=True, stop=False)
+        unread = windows.tile([P, WORDS], F32, name="unread")
+        for warm_up in range(WARM_UPS):
+            nc.tensor.matmul(unread[:], zeros[:, :P], zeros[:], start=True, stop=True)
 
-        for b in range(BLOCKS):
+        window = [windows.tile([P, WORDS], F32, name=f"window{b}") for b in range(BLOCKS)]
+
+        def fill(b, pieces):
+            width = WORDS // pieces
+            for i in range(pieces):
+                columns = slice(i * width, (i + 1) * width)
+                nc.tensor.matmul(
+                    window[b][:, columns], identity[:], base_rows[b][:, columns], start=i == 0, stop=False
+                )
+
+        def add_candidates(b):
             for a in range(K_BLOCKS):
                 nc.tensor.matmul(
                     window[b][:].indirect(offsets[:]),
-                    w_blocks[:, a, b * P : (b + 1) * P],
+                    w_blocks[b][:, a, :],
                     x_blocks[:, a, :],
                     start=False,
                     stop=a == K_BLOCKS - 1,
                 )
 
-        for b in range(BLOCKS):
-            z = window[b][:].rearrange("p (v d) -> p v d", d=SLATE)
+        fill(0, pieces=1)
+        add_candidates(0)
+        for b in range(1, BLOCKS):
+            fill(b, pieces=PIECES)
+        for b in range(1, BLOCKS):
+            add_candidates(b)
+
+        def find_maxima(b):
             slate_max = work.tile([P, SLATES], F32, name="slate_max")
-            nc.vector.tensor_reduce(slate_max[:], z, X_AXIS, OP.max)
+            nc.vector.tensor_reduce(slate_max[:], scores[b], X_AXIS, OP.max)
+            return slate_max
+
+        def exponentiate(b, slate_max):
             shifted = work.tile([P, SLATES, SLATE], F32, name="shifted")
-            nc.vector.tensor_tensor(shifted[:], z, spread(slate_max[:]), OP.subtract)
+            if b == BLOCKS - 2:
+                scores_copy = work.tile([P, SLATES, SLATE], F32, name="scores_copy")
+                nc.scalar.copy(scores_copy[:], scores[b])
+                nc.gpsimd.tensor_tensor(shifted[:], scores_copy[:], spread(slate_max[:]), OP.subtract)
+            else:
+                nc.vector.tensor_tensor(shifted[:], scores[b], spread(slate_max[:]), OP.subtract)
             exps = work.tile([P, SLATES, SLATE], F32, name="exps")
             nc.scalar.activation(exps[:], shifted[:], EXP)
+            return exps
+
+        def normalise_and_store(b, exps):
             slate_sum = work.tile([P, SLATES], F32, name="slate_sum")
             nc.vector.tensor_reduce(slate_sum[:], exps[:], X_AXIS, OP.add)
             inverse = work.tile([P, SLATES], F32, name="inverse")
             nc.vector.reciprocal(inverse[:], slate_sum[:])
-            probs = work.tile([P, SLATES, SLATE], F32, name="probs")
-            normaliser = nc.gpsimd if b < BLOCKS - 1 else nc.vector
-            normaliser.tensor_tensor(probs[:], exps[:], spread(inverse[:]), OP.mult)
-            nc.sync.dma_start(out[b * P : (b + 1) * P, :], probs[:].rearrange("p v d -> p (v d)"))
+            last = b == BLOCKS - 1
+            normaliser = nc.vector if last else nc.gpsimd
+            parts = 2 if last else 1
+            slates = SLATES // parts
+            for i in range(parts):
+                probs = work.tile([P, slates, SLATE], F32, name="last_probs" if last else "probs")
+                some = slice(i * slates, (i + 1) * slates)
+                normaliser.tensor_tensor(
+                    probs[:], exps[:, some, :], inverse[:, some].unsqueeze(2).to_broadcast(probs.shape), OP.mult
+                )
+                words = slice(i * slates * SLATE, (i + 1) * slates * SLATE)
+                nc.sync.dma_start(out[b * P : (b + 1) * P, words], probs[:].rearrange("p v d -> p (v d)"))
+
+        scores = [window[b][:].rearrange("p (v d) -> p v d", d=SLATE) for b in range(BLOCKS)]
+        maxima, exponentials = {}, {}
+        for step in range(BLOCKS + 2):
+            if step < BLOCKS:
+                maxima[step] = find_maxima(step)
+            if 1 <= step <= BLOCKS:
+                exponentials[step - 1] = exponentiate(step - 1, maxima[step - 1])
+            if step >= 2:
+                normalise_and_store(step - 2, exponentials[step - 2])

import concourse.mybir as mybir
from concourse.masks import make_identity

P = 128
STATES, WORDS = 512, 512
FEATURES, CANDIDATES = 256, 128
SLATE = 16
SLATES = WORDS // SLATE
BLOCKS = STATES // P
K_BLOCKS = FEATURES // P

WARM_UPS = 3
SEPARATORS = 24
PIECES = SEPARATORS // (BLOCKS - 1)

FLOPS = 2 * FEATURES * STATES * CANDIDATES + 5 * STATES * WORDS

BF16, F32, U16 = mybir.dt.bfloat16, mybir.dt.float32, mybir.dt.uint16
X_AXIS = mybir.AxisListType.X
OP = mybir.AluOpType
EXP = mybir.ActivationFunctionType.Exp


def spread(per_slate):
    return per_slate.unsqueeze(2).to_broadcast([P, SLATES, SLATE])


def by_slate(row):
    return row.rearrange("p (v d) -> p v d", d=SLATE)


def tile_rows_rescore_kernel(tc, base, x, w, offs, out):
    nc = tc.nc
    with (
        tc.tile_pool(name="held", bufs=1) as held,
        tc.tile_pool(name="work", bufs=BLOCKS) as work,
        tc.psum_pool(name="windows", bufs=1) as windows,
    ):
        base_rows = [held.tile([P, WORDS], BF16, name=f"base_rows{b}") for b in range(BLOCKS)]
        offsets = held.tile([P, CANDIDATES // 16], U16, name="offsets")
        x_blocks = held.tile([P, K_BLOCKS, CANDIDATES], BF16, name="x_blocks")
        w_blocks = [held.tile([P, K_BLOCKS, P], BF16, name="w_first")]
        w_rest = held.tile([P, K_BLOCKS, STATES - P], BF16, name="w_rest")
        w_blocks += [w_rest[:, :, (b - 1) * P : b * P] for b in range(1, BLOCKS)]
        nc.sync.dma_start(base_rows[0][:], base[:P, :])
        nc.sync.dma_start(x_blocks[:], x.rearrange("(a p) n -> p a n", p=P))
        w_by_feature = w.rearrange("(a p) m -> p a m", p=P)
        nc.sync.dma_start(w_blocks[0][:], w_by_feature[:, :, :P])
        nc.sync.dma_start(offsets[:], offs)
        for b in range(1, BLOCKS):
            nc.sync.dma_start(base_rows[b][:], base[b * P : (b + 1) * P, :])
        nc.sync.dma_start(w_rest[:], w_by_feature[:, :, P:])

        zero = held.tile([P, 1], F32, name="zero")
        nc.vector.memset(zero[:], 0.0)
        one = held.tile([P, 1], F32, name="one")
        nc.scalar.activation(one[:], zero[:], EXP)

        zeros = held.tile([P, WORDS], BF16, name="zeros")
        nc.gpsimd.memset(zeros[:], 0.0)
        identity = held.tile([P, P], BF16, name="identity")
        make_identity(nc, identity[:])

        unread = windows.tile([P, WORDS], F32, name="unread")
        for warm_up in range(WARM_UPS):
            nc.tensor.matmul(unread[:], zeros[:, :P], zeros[:], start=True, stop=True)

        window = [windows.tile([P, WORDS], F32, name=f"window{b}") for b in range(BLOCKS)]

        def fill(b, pieces):
            width = WORDS // pieces
            for i in range(pieces):
                columns = slice(i * width, (i + 1) * width)
                nc.tensor.matmul(
                    window[b][:, columns], identity[:], base_rows[b][:, columns], start=i == 0, stop=False
                )

        def add_candidates(b):
            for a in range(K_BLOCKS):
                nc.tensor.matmul(
                    window[b][:].indirect(offsets[:]),
                    w_blocks[b][:, a, :],
                    x_blocks[:, a, :],
                    start=False,
                    stop=a == K_BLOCKS - 1,
                )

        fill(0, pieces=1)
        add_candidates(0)
        for b in range(1, BLOCKS):
            fill(b, pieces=PIECES)
        for b in range(1, BLOCKS):
            add_candidates(b)

        def find_maxima(b):
            slate_max = work.tile([P, SLATES], F32, name="slate_max")
            nc.vector.tensor_reduce(slate_max[:], scores[b], X_AXIS, OP.max)
            return slate_max

        def exponentiate(b, slate_max):
            shifted = work.tile([P, SLATES, SLATE], F32, name="shifted")
            if b == BLOCKS - 2:
                scores_copy = work.tile([P, SLATES, SLATE], F32, name="scores_copy")
                nc.scalar.copy(scores_copy[:], scores[b])
                nc.gpsimd.tensor_tensor(shifted[:], scores_copy[:], spread(slate_max[:]), OP.subtract)
            else:
                nc.vector.tensor_tensor(shifted[:], scores[b], spread(slate_max[:]), OP.subtract)
            exps = work.tile([P, SLATES, SLATE], F32, name="exps")
            nc.scalar.activation(exps[:], shifted[:], EXP)
            return exps

        def normalise_and_store(b, exps):
            slate_sum = work.tile([P, SLATES], F32, name="slate_sum")
            nc.vector.tensor_reduce(slate_sum[:], exps[:], X_AXIS, OP.add)
            inverse = work.tile([P, SLATES], F32, name="inverse")
            nc.vector.reciprocal(inverse[:], slate_sum[:])
            last = b == BLOCKS - 1
            normaliser = nc.vector if last else nc.gpsimd
            parts = 2 if last else 1
            slates = SLATES // parts
            for i in range(parts):
                probs = work.tile([P, slates, SLATE], F32, name="last_probs" if last else "probs")
                some = slice(i * slates, (i + 1) * slates)
                normaliser.tensor_tensor(
                    probs[:], exps[:, some, :], inverse[:, some].unsqueeze(2).to_broadcast(probs.shape), OP.mult
                )
                words = slice(i * slates * SLATE, (i + 1) * slates * SLATE)
                nc.sync.dma_start(out[b * P : (b + 1) * P, words], probs[:].rearrange("p v d -> p (v d)"))

        scores = [window[b][:].rearrange("p (v d) -> p v d", d=SLATE) for b in range(BLOCKS)]
        maxima, exponentials = {}, {}
        for step in range(BLOCKS + 2):
            if step < BLOCKS:
                maxima[step] = find_maxima(step)
            if 1 <= step <= BLOCKS:
                exponentials[step - 1] = exponentiate(step - 1, maxima[step - 1])
            if step >= 2:
                normalise_and_store(step - 2, exponentials[step - 2])
